import numpy as np, ml_dtypes
CORES = [2,130,10,138,18,146,26,154,34,162,42,170,50,178,58,186]
N = 16
ROOT = 3
WIDTHS = [4,8,0,0,0,8,8,4,0,0,8,0,4,4,0,0]
OFF = [0,4,12,12,12,12,20,28,32,32,32,40,40,44,48,48]
C = 48
def setup_inputs(rng):
    return {"x": rng.standard_normal((N, 128, C), dtype=np.float32).astype(ml_dtypes.bfloat16)}
def reference(x):
    YW = max(WIDTHS)
    y = np.full((N, 128, YW), np.nan, x.dtype)
    for r in range(N):
        y[r][:, :WIDTHS[r]] = x[ROOT][:, OFF[r]:OFF[r] + WIDTHS[r]]
    return {"y": y}

@@ -1,0 +1,43 @@
+from concourse.bass import DstId, RemoteDMATransfer
+
+SCRATCH = {
+    "blk": ("dram", [128, 48], "bfloat16"),
+}
+SEMAPHORES = ["loaded", "sent", "arrived", "stored"]
+
+
+def rank_program(g, core, T, topo):
+    rank = T.rank_of(core)
+    if rank is None:
+        return
+    widths, off = T.tables["WIDTHS"], T.tables["OFF"]
+    root = T.root
+
+    if rank == root:
+        dests = [r for r in range(len(T.cores)) if widths[r] > 0 and r != root]
+        g.sync.dma_start(T.blk[:], T.x[:]).then_inc(T.sem.loaded, 16)
+        g.wait_ge(T.sem.loaded, 16)
+        left = 0
+        for i in range(0, len(dests), 8):
+            transfers = []
+            for k, r in enumerate(dests[i:i + 8]):
+                rid, pid = topo.addr(T.cores[r], core)
+                transfers.append(RemoteDMATransfer(
+                    dst_ids=[DstId(rid=rid, pnc=pid)], dma_engine_mask=1 << k,
+                    remote_sem=T.sem.arrived, src=T.blk[:], dst=T.blk[:]))
+            g.remote_dma_fused(transfers, local_sem=T.sem.sent)
+            left += len(transfers)
+        if widths[root] > 0:
+            w, o = widths[root], off[root]
+            g.sync.wait_ge(T.sem.loaded, 16)
+            g.sync.dma_start(T.y[:, 0:w], T.blk[:, o:o + w]).then_inc(T.sem.stored, 16)
+            g.sync.wait_ge(T.sem.stored, 16)
+        g.wait_ge(T.sem.sent, left)
+        return
+
+    w, o = widths[rank], off[rank]
+    if w == 0:
+        return
+    g.sync.wait_ge(T.sem.arrived, 1)
+    g.sync.dma_start(T.y[:, 0:w], T.blk[:, o:o + w]).then_inc(T.sem.stored, 16)
+    g.sync.wait_ge(T.sem.stored, 16)

@@ -1,7 +1,8 @@
 from concourse.bass import DstId, RemoteDMATransfer
 
+WD = 28
 SCRATCH = {
-    "blk": ("dram", [128, 48], "bfloat16"),
+    "win": ("dram", [2, 128, WD], "bfloat16"),
 }
 SEMAPHORES = ["loaded", "sent", "arrived", "stored"]
 
@@ -10,34 +11,34 @@ def rank_program(g, core, T, topo):
     rank = T.rank_of(core)
     if rank is None:
         return
-    widths, off = T.tables["WIDTHS"], T.tables["OFF"]
+    widths, off, C = T.tables["WIDTHS"], T.tables["OFF"], T.tables["C"]
     root = T.root
+    base = [0, C - WD]
+
+    def window(r):
+        return 0 if off[r] + widths[r] <= WD else 1
 
     if rank == root:
         dests = [r for r in range(len(T.cores)) if widths[r] > 0 and r != root]
-        g.sync.dma_start(T.blk[:], T.x[:]).then_inc(T.sem.loaded, 16)
-        g.wait_ge(T.sem.loaded, 16)
-        left = 0
-        for i in range(0, len(dests), 8):
-            transfers = []
-            for k, r in enumerate(dests[i:i + 8]):
-                rid, pid = topo.addr(T.cores[r], core)
-                transfers.append(RemoteDMATransfer(
-                    dst_ids=[DstId(rid=rid, pnc=pid)], dma_engine_mask=1 << k,
-                    remote_sem=T.sem.arrived, src=T.blk[:], dst=T.blk[:]))
-            g.remote_dma_fused(transfers, local_sem=T.sem.sent)
-            left += len(transfers)
-        if widths[root] > 0:
-            w, o = widths[root], off[root]
-            g.sync.wait_ge(T.sem.loaded, 16)
-            g.sync.dma_start(T.y[:, 0:w], T.blk[:, o:o + w]).then_inc(T.sem.stored, 16)
-            g.sync.wait_ge(T.sem.stored, 16)
-        g.wait_ge(T.sem.sent, left)
+        g.sync.dma_start(T.win[0], T.x[:, 0:WD]).then_inc(T.sem.loaded, 16)
+        g.scalar.dma_start(T.win[1], T.x[:, C - WD:C]).then_inc(T.sem.loaded, 16)
+        g.wait_ge(T.sem.loaded, 32)
+        transfers = []
+        for k, r in enumerate(dests):
+            rid, pid = topo.addr(T.cores[r], core)
+            j = window(r)
+            transfers.append(RemoteDMATransfer(
+                dst_ids=[DstId(rid=rid, pnc=pid)], dma_engine_mask=1 << k,
+                remote_sem=T.sem.arrived, src=T.win[j], dst=T.win[j]))
+        g.remote_dma_fused(transfers, local_sem=T.sem.sent)
+        g.wait_ge(T.sem.sent, len(transfers))
         return
 
-    w, o = widths[rank], off[rank]
+    w = widths[rank]
     if w == 0:
         return
+    j = window(rank)
+    o = off[rank] - base[j]
     g.sync.wait_ge(T.sem.arrived, 1)
-    g.sync.dma_start(T.y[:, 0:w], T.blk[:, o:o + w]).then_inc(T.sem.stored, 16)
+    g.sync.dma_start(T.y[:, 0:w], T.win[j, :, o:o + w]).then_inc(T.sem.stored, 16)
     g.sync.wait_ge(T.sem.stored, 16)

@@ -24,14 +24,17 @@ def rank_program(g, core, T, topo):
         g.scalar.dma_start(T.win[1], T.x[:, C - WD:C]).then_inc(T.sem.loaded, 16)
         g.wait_ge(T.sem.loaded, 32)
         transfers = []
-        for k, r in enumerate(dests):
-            rid, pid = topo.addr(T.cores[r], core)
-            j = window(r)
+        for j in range(2):
+            ds = [r for r in dests if window(r) == j]
+            ids = []
+            for r in ds:
+                rid, pid = topo.addr(T.cores[r], core)
+                ids.append(DstId(rid=rid, pnc=pid))
             transfers.append(RemoteDMATransfer(
-                dst_ids=[DstId(rid=rid, pnc=pid)], dma_engine_mask=1 << k,
-                remote_sem=T.sem.arrived, src=T.win[j], dst=T.win[j]))
+                dst_ids=ids, dma_engine_mask=0xF << (4 * j),
+                remote_sem=T.sem.arrived, srcs=[T.win[j]], dsts=[T.win[j] for r in ds]))
         g.remote_dma_fused(transfers, local_sem=T.sem.sent)
-        g.wait_ge(T.sem.sent, len(transfers))
+        g.wait_ge(T.sem.sent, 8)
         return
 
     w = widths[rank]
@@ -39,6 +42,6 @@ def rank_program(g, core, T, topo):
         return
     j = window(rank)
     o = off[rank] - base[j]
-    g.sync.wait_ge(T.sem.arrived, 1)
+    g.sync.wait_ge(T.sem.arrived, 4)
     g.sync.dma_start(T.y[:, 0:w], T.win[j, :, o:o + w]).then_inc(T.sem.stored, 16)
     g.sync.wait_ge(T.sem.stored, 16)

@@ -18,6 +18,14 @@ def rank_program(g, core, T, topo):
     def window(r):
         return 0 if off[r] + widths[r] <= WD else 1
 
+    def links(r):
+        d = T.cores[r]
+        if topo.mates(core, d):
+            return 1
+        if topo.same_plane(core, d):
+            return 2
+        return 3
+
     if rank == root:
         dests = [r for r in range(len(T.cores)) if widths[r] > 0 and r != root]
         g.sync.dma_start(T.win[0], T.x[:, 0:WD]).then_inc(T.sem.loaded, 16)
@@ -25,7 +33,7 @@ def rank_program(g, core, T, topo):
         g.wait_ge(T.sem.loaded, 32)
         transfers = []
         for j in range(2):
-            ds = [r for r in dests if window(r) == j]
+            ds = sorted([r for r in dests if window(r) == j], key=lambda r: -links(r))
             ids = []
             for r in ds:
                 rid, pid = topo.addr(T.cores[r], core)

from concourse.bass import DstId, RemoteDMATransfer

WD = 28
SCRATCH = {
    "win": ("dram", [2, 128, WD], "bfloat16"),
}
SEMAPHORES = ["loaded", "sent", "arrived", "stored"]


def rank_program(g, core, T, topo):
    rank = T.rank_of(core)
    if rank is None:
        return
    widths, off, C = T.tables["WIDTHS"], T.tables["OFF"], T.tables["C"]
    root = T.root
    base = [0, C - WD]

    def window(r):
        return 0 if off[r] + widths[r] <= WD else 1

    def links(r):
        d = T.cores[r]
        if topo.mates(core, d):
            return 1
        if topo.same_plane(core, d):
            return 2
        return 3

    if rank == root:
        dests = [r for r in range(len(T.cores)) if widths[r] > 0 and r != root]
        g.sync.dma_start(T.win[0], T.x[:, 0:WD]).then_inc(T.sem.loaded, 16)
        g.scalar.dma_start(T.win[1], T.x[:, C - WD:C]).then_inc(T.sem.loaded, 16)
        g.wait_ge(T.sem.loaded, 32)
        transfers = []
        for j in range(2):
            ds = sorted([r for r in dests if window(r) == j], key=lambda r: -links(r))
            ids = []
            for r in ds:
                rid, pid = topo.addr(T.cores[r], core)
                ids.append(DstId(rid=rid, pnc=pid))
            transfers.append(RemoteDMATransfer(
                dst_ids=ids, dma_engine_mask=0xF << (4 * j),
                remote_sem=T.sem.arrived, srcs=[T.win[j]], dsts=[T.win[j] for r in ds]))
        g.remote_dma_fused(transfers, local_sem=T.sem.sent)
        g.wait_ge(T.sem.sent, 8)
        return

    w = widths[rank]
    if w == 0:
        return
    j = window(rank)
    o = off[rank] - base[j]
    g.sync.wait_ge(T.sem.arrived, 4)
    g.sync.dma_start(T.y[:, 0:w], T.win[j, :, o:o + w]).then_inc(T.sem.stored, 16)
    g.sync.wait_ge(T.sem.stored, 16)
